import numpy as np
import ml_dtypes


def mxq(x, axis, fmt="e4m3"):
    dtype, down = {"e4m3": (ml_dtypes.float8_e4m3fn, 7), "e5m2": (ml_dtypes.float8_e5m2, 14)}[fmt]
    v = np.moveaxis(np.asarray(x, np.float32).astype(ml_dtypes.bfloat16).astype(np.float64), axis, -1)
    blocks = v.reshape(v.shape[:-1] + (-1, 32))
    amax = np.abs(blocks).max(-1, keepdims=True)
    byte = np.maximum(np.where(amax > 0, np.frexp(amax)[1] - 1 + 127, 0) - down, 1)
    scale = np.exp2(byte - 127.0)
    codes = (blocks / scale).astype(np.float32).astype(dtype).astype(np.float64)
    return np.moveaxis((codes * scale).reshape(v.shape), -1, axis)


WIDE = False


def mx_kscale(k):
    if not WIDE:
        return np.ones(k)
    levels = np.array([10, -10, 5, -5, 0])
    if k % 512:
        return np.exp2(np.random.permutation(np.resize(levels, k // 32))).repeat(32)
    a = np.empty((k // 512, 16))
    for p in range(k // 512):
        a[p, :8] = np.random.permutation(np.resize(levels, 8))
        for g in range(8):
            far = levels[np.abs(levels - a[p, g]) >= 10]
            a[p, g + 8] = far[np.random.randint(len(far))]
    return np.exp2(a.ravel()).repeat(32)


def f64(x):
    return np.asarray(x).astype(np.float64)


def striped(idx):
    return np.tile(idx.reshape(-1, 16).T, (8, 1)).astype(np.uint16)


def unstriped(offs):
    return offs[:16].T.reshape(-1).astype(np.int64)


E2M1 = np.array([0.0, 0.5, 1.0, 1.5, 2.0, 3.0, 4.0, 6.0, -0.0, -0.5, -1.0, -1.5, -2.0, -3.0, -4.0, -6.0])


def pack_weight(w, fmt):
    k, n = w.shape
    w = f64(np.asarray(w, np.float32).astype(ml_dtypes.bfloat16)).reshape(k // 32, 32, n)
    amax = np.abs(w).max(1)
    if fmt == "e4m3":
        byte = np.frexp(amax)[1] - 1 + 127 - 7
    else:
        mant, ex = np.frexp(amax / 6.0)
        byte = np.where(mant > 0.5, ex, ex - 1) + 127
    byte = np.clip(np.where(amax > 0, byte, 1), 1, 254)
    scaled = (w * np.exp2(127.0 - byte)[:, None, :]).reshape(k, n).astype(np.float32)
    by_word = np.ascontiguousarray(scaled.reshape(k // 512, 128, 4, n).transpose(0, 1, 3, 2))
    if fmt == "e4m3":
        words = by_word.astype(ml_dtypes.float8_e4m3fn).view(np.uint8)
    else:
        c = by_word.astype(ml_dtypes.float4_e2m1fn).view(np.uint8) & 0xF
        words = (c[..., 0::2] | (c[..., 1::2] << 4)).reshape(k // 512, 128, 2 * n)
    return np.ascontiguousarray(words), np.ascontiguousarray(byte.astype(np.uint8).reshape(k // 512, 16, n))


def unpack_weight(words, scales, fmt):
    g, _, n = scales.shape
    words = np.ascontiguousarray(words).reshape(g, 128, n, -1)
    if fmt == "e4m3":
        vals = words.view(ml_dtypes.float8_e4m3fn).astype(np.float64)
    else:
        nib = np.empty((g, 128, n, 4), np.uint8)
        nib[..., 0::2] = words & 0xF
        nib[..., 1::2] = words >> 4
        vals = E2M1[nib]
    vals = vals * np.repeat(np.exp2(scales.astype(np.float64) - 127.0), 8, axis=1)[..., None]
    return vals.transpose(0, 1, 3, 2).reshape(g * 512, n)


def gelu(v):
    return 0.5 * v * (1.0 + np.tanh(np.sqrt(2.0 / np.pi) * (v + 0.044715 * v**3)))


def twice(P):
    return np.random.permutation(np.repeat(np.arange(P), 2))


def bf(x):
    return np.asarray(x, np.float32).astype(ml_dtypes.bfloat16)


def planes(Y):
    n, m = Y.shape
    b = f64(bf(Y)).reshape(n // 32, 32, m)
    amax = np.abs(b).max(1)
    byte = np.clip(np.where(amax > 0, np.frexp(amax)[1] - 1 + 127 - 7, 1), 1, 254)
    codes = (b * np.exp2(127.0 - byte)[:, None, :]).reshape(n, m).astype(np.float32).astype(ml_dtypes.float8_e4m3fn).view(np.uint8)
    words = codes.reshape(n // 512, 128, 4, m).transpose(0, 1, 3, 2)
    return np.ascontiguousarray(words), np.ascontiguousarray(byte.astype(np.uint8).reshape(n // 512, 16, m))


K, H, T, S, P = 1536, 1024, 4096, 1024, 512

def setup_inputs():
    n = np.random.standard_normal
    s = mx_kscale(K)[:, None]
    u = mx_kscale(H)[:, None]
    d = {}
    d["tab_words"], d["tab_scales"] = pack_weight(n((K, T)) * s, "e4m3")
    d["offs"] = striped(np.random.permutation(T)[:S])
    d["w1"] = (n((K, H)) / K ** 0.5 / s * u.T).astype(np.float32)
    d["b1"] = (0.5 * n(H) * u[:, 0]).astype(np.float32)
    d["pos1"] = striped(np.random.permutation(S)[:P])
    d["pos2"] = striped(np.random.permutation(S)[:P])
    d["w2_words"], d["w2_scales"] = pack_weight(0.8 * n((H, H)) / H ** 0.5 / u, "e2m1")
    d["w3"] = (0.8 * n((H, H)) / H ** 0.5 / u).astype(np.float32)
    d["pos3"] = striped(twice(P))
    d["gain"] = (0.8 * np.exp(0.3 * n(H)) / u[:, 0]).astype(np.float32)
    d["amp"] = np.exp(0.8 * n(H)).astype(np.float32)
    return d

def reference(tab_words, tab_scales, offs, w1, b1, pos1, pos2, w2_words, w2_scales, w3, pos3, gain, amp):
    v = unpack_weight(tab_words, tab_scales, "e4m3")[:, unstriped(offs)]
    h = (mxq(f64(w1), 0, "e4m3").T @ v) + f64(b1)[:, None]
    ha = h[:, unstriped(pos1)]
    hb = h[:, unstriped(pos2)]
    hi = mxq(np.maximum(ha, hb), 0, "e4m3")
    lo = mxq(np.minimum(ha, hb), 0, "e4m3")
    w2 = unpack_weight(w2_words, w2_scales, "e2m1")
    tree = w2.T @ hi + mxq(f64(w3), 0, "e4m3").T @ lo
    x = tree[:, unstriped(pos3)] + f64(gain)[:, None] * h
    y = f64(amp)[:, None] * (0.5 * x * (1.0 + np.tanh(0.7978845608028654 * (x + 0.044715 * x ** 3))))
    words, scales = planes(y)
    return y, words, scales

@@ -1,0 +1,283 @@
+from contextlib import ExitStack
+
+import concourse.mybir as mybir
+
+K, H, T, S, M = 1536, 1024, 4096, 1024, 512
+FLOPS = 2 * K * H * S + 2 * 2 * H * H * M
+
+F32 = mybir.dt.float32
+BF16 = mybir.dt.bfloat16
+I32 = mybir.dt.int32
+U32 = mybir.dt.uint32
+U16 = mybir.dt.uint16
+U8 = mybir.dt.uint8
+FP8X4 = mybir.dt.float8_e4m3fn_x4
+FP4X4 = mybir.dt.float4_e2m1fn_x4
+ACT = mybir.ActivationFunctionType
+ALU = mybir.AluOpType
+
+P = 128
+PACK = 4
+GROUP = P * PACK
+K_PASSES = K // GROUP
+H_GROUPS = H // GROUP
+BANK = 512
+TREE_PAD = 16
+Y_CHUNKS = [[(0, 512), (512, 512)], [(0, 512), (512, 256), (768, 256)]]
+
+
+def tile_list_tree_ring_dating_kernel(
+    tc, tab_words, tab_scales, offs, w1, b1, pos1, pos2, w2_words, w2_scales, w3, pos3, gain, amp,
+    out_0, out_1, out_2,
+):
+    nc = tc.nc
+    with ExitStack() as ctx:
+        lists = ctx.enter_context(tc.tile_pool(name="lists", bufs=1))
+        keep = ctx.enter_context(tc.tile_pool(name="keep", bufs=1))
+        ring = ctx.enter_context(tc.tile_pool(name="ring", bufs=1))
+        psum = ctx.enter_context(tc.psum_pool(name="psum", bufs=1))
+
+        def load_list(src, name):
+            tile = lists.tile(list(src.shape), U16, name=name)
+            nc.sync.dma_start(tile[:], src)
+            return tile
+
+        def big(shape, dtype, name):
+            return ring.tile(shape, dtype, name=name, tag="big", bufs=3, align_bytes=64)
+
+        def raw(shape, name, dtype=F32):
+            return ring.tile(shape, dtype, name=name, tag="raw", bufs=3, align_bytes=64)
+
+        def small(shape, dtype, name):
+            return ring.tile(shape, dtype, name=name, tag="small", bufs=5, align_bytes=64)
+
+        def mx_pair(width, name):
+            codes = keep.tile([P, width], U32, name=name + "_codes", align_bytes=64)
+            scales = keep.tile([P, width], U8, name=name + "_scales", align_bytes=64)
+            return codes, scales
+
+        def quantize(pair, staged, first, width):
+            codes, scales = pair
+            nc.vector.quantize_mx(
+                out=codes[:, first:first + width].bitcast(FP8X4),
+                scales=scales[:, first:first + width],
+                in_=staged,
+            )
+
+        def deal(copy, staged, rows, m0, m1):
+            copy(
+                out=staged.rearrange("p (t m j) -> p m j t", t=PACK, j=PACK)[:, m0:m1],
+                in_=rows.rearrange("p j (m t) -> p m j t", t=PACK),
+            )
+
+        def weight_stage(name):
+            return small([P, PACK * GROUP], BF16, name)
+
+        def w1_rows(a, c0, c1):
+            return w1[a * GROUP:(a + 1) * GROUP, c0:c1].rearrange("(p j) c -> p j c", j=PACK)
+
+        def bank(i, name):
+            return psum.tile([P, BANK], F32, name=name, tag="bank%d" % i)
+
+        offs_t = load_list(offs, "offs_t")
+        tab_scale_rows = ring.tile([P, T], U8, name="tab_scale_rows", tag="scale_rows", align_bytes=64)
+        w2_raw = small([P, H_GROUPS, 2 * H], U8, "w2_raw")
+        nc.vector.memset(tab_scale_rows[:].bitcast(I32), 0)
+        for q in range(4):
+            nc.gpsimd.dma_start(
+                tab_scale_rows[32 * q:32 * q + 4 * K_PASSES, :].bitcast(I32),
+                tab_scales[:, 4 * q:4 * q + 4, :].bitcast(I32),
+            )
+
+        def load_vector(src, name):
+            vec = keep.tile([P, H_GROUPS, PACK], F32, name=name)
+            nc.sync.dma_start(vec[:], src.rearrange("(g p t) -> p g t", p=P, t=PACK))
+            return vec
+
+        tree = [[keep.tile([P, M + TREE_PAD], F32, name="tree%d%d" % (g, t)) for t in range(PACK)]
+                for g in range(H_GROUPS)]
+        for g in range(H_GROUPS):
+            for t in range(PACK):
+                nc.vector.memset(tree[g][t][:, M:], 0.0)
+
+        nc.sync.dma_start(w2_raw[:].bitcast(I32), w2_words.rearrange("a p c -> p a c").bitcast(I32))
+
+        w2_codes = keep.tile([P, H_GROUPS * H_GROUPS, PACK, 2 * P], U8, name="w2_codes", align_bytes=64)
+        w2_planes = keep.tile([P, H_GROUPS * H_GROUPS, PACK, P], U8, name="w2_planes", align_bytes=64)
+        nc.vector.tensor_copy(
+            out=w2_codes[:].rearrange("p s t (q b) -> p s q t b", b=2),
+            in_=w2_raw[:].rearrange("p a (g q t b) -> p (a g) q t b", g=H_GROUPS, t=PACK, b=2),
+        )
+
+        v_scales = keep.tile([P, S], U8, name="v_scales", align_bytes=64)
+        nc.vector.tensor_copy(v_scales[:], tab_scale_rows[:].indirect(offs_t[:]))
+        w2_scale_rows = ring.tile([P, H_GROUPS, H], U8, name="w2_scale_rows", tag="scale_rows", align_bytes=64)
+        nc.vector.memset(w2_scale_rows[:].bitcast(I32), 0)
+        for q in range(4):
+            nc.scalar.dma_start(
+                w2_scale_rows[32 * q:32 * q + 4, :, :].bitcast(I32),
+                w2_scales[:, 4 * q:4 * q + 4, :].rearrange("a r c -> r a c").bitcast(I32),
+            )
+        nc.vector.tensor_copy(
+            out=w2_planes[:].rearrange("p s t q -> p s q t"),
+            in_=w2_scale_rows[:].rearrange("p a (g q t) -> p (a g) q t", g=H_GROUPS, t=PACK),
+        )
+        v_words = []
+        w1_mx = [[mx_pair(GROUP, "w1_%d%d" % (g, a)) for a in range(K_PASSES)] for g in range(H_GROUPS)]
+        for a in range(K_PASSES):
+            table = big([P, T], I32, "table%d" % a)
+            nc.sync.dma_start(table[:], tab_words[a].rearrange("p n t -> p (n t)").bitcast(I32))
+            picked = keep.tile([P, S], U32, name="v_words%d" % a, align_bytes=64)
+            nc.vector.tensor_copy(picked[:], table[:].bitcast(U32).indirect(offs_t[:]))
+            v_words.append(picked)
+            staged = weight_stage("w1_bf0%d" % a)
+            if a < K_PASSES - 1:
+                rows = raw([P, PACK, GROUP], "w1_raw0%d" % a)
+                nc.sync.dma_start(rows[:], w1_rows(a, 0, GROUP))
+                deal(nc.scalar.copy, staged[:], rows[:], 0, P)
+                quantize(w1_mx[0][a], staged[:], 0, GROUP)
+            else:
+                for half, copy in enumerate((nc.scalar.copy, nc.vector.tensor_copy)):
+                    rows = raw([P, PACK, GROUP // 2], "w1_raw0%d%d" % (a, half))
+                    nc.sync.dma_start(rows[:], w1_rows(a, half * GROUP // 2, (half + 1) * GROUP // 2))
+                    deal(copy, staged[:], rows[:], half * P // 2, (half + 1) * P // 2)
+                for t in range(PACK):
+                    quantize(w1_mx[0][a], staged[:, t * GROUP:(t + 1) * GROUP], t * P, P)
+            if a == 0:
+                pos1_t = load_list(pos1, "pos1_t")
+                pos2_t = load_list(pos2, "pos2_t")
+                b1_t = load_vector(b1, "b1_t")
+
+        h = [[keep.tile([P, S], F32, name="h%d%d" % (g, t)) for t in range(PACK)] for g in range(H_GROUPS)]
+
+        def stage1_products(g):
+            acc = [[bank(2 * t + c, "h_acc%d%d%d" % (g, t, c)) for c in range(2)] for t in range(PACK)]
+            for a in range(K_PASSES):
+                codes, scales = w1_mx[g][a]
+                for t in range(PACK):
+                    for c in range(2):
+                        cols = slice(c * BANK, (c + 1) * BANK)
+                        nc.tensor.matmul_mx(
+                            out=acc[t][c][:],
+                            lhsT=codes[:, t * P:(t + 1) * P].bitcast(FP8X4),
+                            lhsT_scale=scales[:, t * P:(t + 1) * P],
+                            rhs=v_words[a][:, cols].bitcast(FP8X4),
+                            rhs_scale=v_scales[4 * a:P, cols],
+                            start=(a == 0),
+                            stop=(a == K_PASSES - 1),
+                        )
+            for t in range(PACK):
+                for c in range(2):
+                    cols = slice(c * BANK, (c + 1) * BANK)
+                    bias = b1_t[:, g, t:t + 1]
+                    if g == 0 and t == 0 and c == 1:
+                        nc.vector.tensor_scalar(h[g][t][:, cols], acc[t][c][:], bias, None, ALU.add)
+                    else:
+                        nc.scalar.activation(h[g][t][:, cols], acc[t][c][:], ACT.Identity, bias=bias, scale=1.0)
+
+        hi_mx = [mx_pair(M, "hi%d" % g) for g in range(H_GROUPS)]
+        lo_mx = [mx_pair(M, "lo%d" % g) for g in range(H_GROUPS)]
+
+        def pair_up(g):
+            ha = ring.tile([P, PACK, M], F32, name="ha%d" % g, tag="hab", bufs=2)
+            hb = ring.tile([P, PACK, M], F32, name="hb%d" % g, tag="hab", bufs=2)
+            for t in range(PACK):
+                nc.vector.tensor_copy(ha[:, t, :], h[g][t][:].indirect(pos1_t[:]))
+                nc.vector.tensor_copy(hb[:, t, :], h[g][t][:].indirect(pos2_t[:]))
+            staged = []
+            for op, name in ((ALU.max, "hi"), (ALU.min, "lo")):
+                both = small([P, PACK * M], BF16, "%s_bf%d" % (name, g))
+                nc.vector.tensor_tensor(
+                    out=both[:].rearrange("p (c i t) -> p c t i", i=4, t=PACK),
+                    in0=ha[:].rearrange("p t (c i) -> p c t i", i=4),
+                    in1=hb[:].rearrange("p t (c i) -> p c t i", i=4),
+                    op=op,
+                )
+                staged.append(both)
+            quantize(hi_mx[g], staged[0][:], 0, M)
+            quantize(lo_mx[g], staged[1][:], 0, M)
+
+        stage1_products(0)
+
+        for a in range(K_PASSES):
+            rows = raw([P, PACK, GROUP], "w1_raw1%d" % a)
+            nc.sync.dma_start(rows[:], w1_rows(a, GROUP, 2 * GROUP))
+            staged = weight_stage("w1_bf1%d" % a)
+            deal(nc.scalar.copy, staged[:], rows[:], 0, P)
+            quantize(w1_mx[1][a], staged[:], 0, GROUP)
+        stage1_products(1)
+        pair_up(0)
+        pos3_t = load_list(pos3, "pos3_t")
+        gain_t = load_vector(gain, "gain_t")
+        amp_t = load_vector(amp, "amp_t")
+
+        w3_mx = [mx_pair(H, "w3_%d" % a) for a in range(H_GROUPS)]
+        for a in range(H_GROUPS):
+            rows = big([P, PACK, H], F32, "w3_raw%d" % a)
+            nc.sync.dma_start(rows[:], w3[a * GROUP:(a + 1) * GROUP, :].rearrange("(p j) c -> p j c", j=PACK))
+            staged = raw([P, H_GROUPS, PACK * GROUP], "w3_bf%d" % a, BF16)
+            for g in range(H_GROUPS):
+                deal(nc.scalar.copy, staged[:, g, :], rows[:, :, g * GROUP:(g + 1) * GROUP], 0, P)
+            quantize(w3_mx[a], staged[:].rearrange("p g c -> p (g c)"), 0, H)
+        pair_up(1)
+
+        acc = [[bank(PACK * g + t, "tree_acc%d%d" % (g, t)) for t in range(PACK)] for g in range(H_GROUPS)]
+        for a in range(H_GROUPS):
+            for g in range(H_GROUPS):
+                for t in range(PACK):
+                    nc.tensor.matmul_mx(
+                        out=acc[g][t][:],
+                        lhsT=w2_codes[:, H_GROUPS * a + g, t, :].bitcast(FP4X4),
+                        lhsT_scale=w2_planes[:, H_GROUPS * a + g, t, :],
+                        rhs=hi_mx[a][0][:].bitcast(FP8X4),
+                        rhs_scale=hi_mx[a][1][:],
+                        start=(a == 0),
+                        stop=False,
+                    )
+            for g in range(H_GROUPS):
+                codes, scales = w3_mx[a]
+                for t in range(PACK):
+                    chans = slice((PACK * g + t) * P, (PACK * g + t + 1) * P)
+                    nc.tensor.matmul_mx(
+                        out=acc[g][t][:],
+                        lhsT=codes[:, chans].bitcast(FP8X4),
+                        lhsT_scale=scales[:, chans],
+                        rhs=lo_mx[a][0][:].bitcast(FP8X4),
+                        rhs_scale=lo_mx[a][1][:],
+                        start=False,
+                        stop=(a == H_GROUPS - 1),
+                    )
+
+        for g in range(H_GROUPS):
+            for t in range(PACK):
+                nc.scalar.copy(tree[g][t][:, :M], acc[g][t][:])
+            y = big([P, PACK, S], F32, "y%d" % g)
+            y_mx = mx_pair(S, "y%d" % g)
+            y_rows = out_0[g * GROUP:(g + 1) * GROUP, :].rearrange("(p t) c -> p t c", t=PACK)
+            y_words = out_1[g].rearrange("p n t -> p (n t)").bitcast(I32)
+            for first, width in Y_CHUNKS[g]:
+                cols = slice(first, first + width)
+                last = g == H_GROUPS - 1 and first + width == S
+                for t in range(PACK):
+                    x = ring.tile([P, width], F32, name="x%d%d%d" % (g, first, t), tag="x", bufs=4)
+                    nc.vector.tensor_copy(x[:], tree[g][t][:].indirect(pos3_t[:, first // 16:(first + width) // 16]))
+                    nc.vector.scalar_tensor_tensor(
+                        out=x[:], in0=h[g][t][:, cols], scalar=gain_t[:, g, t:t + 1], in1=x[:],
+                        op0=ALU.mult, op1=ALU.add,
+                    )
+                    nc.scalar.activation(y[:, t, cols], x[:], ACT.Gelu_apprx_tanh)
+                    nc.scalar.activation(y[:, t, cols], y[:, t, cols], ACT.Copy, scale=amp_t[:, g, t:t + 1])
+                nc.sync.dma_start(y_rows[:, :, cols], y[:, :, cols])
+                staged = small([P, PACK * width], BF16, "y_bf%d%d" % (g, first))
+                copy = nc.vector.tensor_copy if last else nc.scalar.copy
+                copy(
+                    out=staged[:].rearrange("p (c i t) -> p c t i", i=4, t=PACK),
+                    in_=y[:, :, cols].rearrange("p t (c i) -> p c t i", i=4),
+                )
+                quantize(y_mx, staged[:], first, width)
+                nc.sync.dma_start(y_words[:, cols], y_mx[0][:, cols].bitcast(I32))
+            for q in range(4):
+                nc.sync.dma_start(
+                    out_2[g, 4 * q:4 * q + 4, :].bitcast(I32),
+                    y_mx[1][32 * q:32 * q + 4, :].bitcast(I32),
+                )

@@ -49,7 +49,7 @@ def tile_list_tree_ring_dating_kernel(
             return ring.tile(shape, dtype, name=name, tag="raw", bufs=3, align_bytes=64)
 
         def small(shape, dtype, name):
-            return ring.tile(shape, dtype, name=name, tag="small", bufs=5, align_bytes=64)
+            return ring.tile(shape, dtype, name=name, tag="small", bufs=6, align_bytes=64)
 
         def mx_pair(width, name):
             codes = keep.tile([P, width], U32, name=name + "_codes", align_bytes=64)
@@ -80,14 +80,21 @@ def tile_list_tree_ring_dating_kernel(
             return psum.tile([P, BANK], F32, name=name, tag="bank%d" % i)
 
         offs_t = load_list(offs, "offs_t")
-        tab_scale_rows = ring.tile([P, T], U8, name="tab_scale_rows", tag="scale_rows", align_bytes=64)
+        tab_scale_rows = small([P, T], U8, "tab_scale_rows")
+        w2_scale_rows = small([P, H_GROUPS, H], U8, "w2_scale_rows")
         w2_raw = small([P, H_GROUPS, 2 * H], U8, "w2_raw")
         nc.vector.memset(tab_scale_rows[:].bitcast(I32), 0)
-        for q in range(4):
-            nc.gpsimd.dma_start(
-                tab_scale_rows[32 * q:32 * q + 4 * K_PASSES, :].bitcast(I32),
-                tab_scales[:, 4 * q:4 * q + 4, :].bitcast(I32),
-            )
+        nc.vector.memset(w2_scale_rows[:].bitcast(I32), 0)
+
+        def load_table(a):
+            table = big([P, T], I32, "table%d" % a)
+            nc.sync.dma_start(table[:], tab_words[a].rearrange("p n t -> p (n t)").bitcast(I32))
+            return table
+
+        def load_w1(g, a, c0, c1):
+            rows = raw([P, PACK, c1 - c0], "w1_raw%d%d%d" % (g, a, c0))
+            nc.sync.dma_start(rows[:], w1_rows(a, g * GROUP + c0, g * GROUP + c1))
+            return rows
 
         def load_vector(src, name):
             vec = keep.tile([P, H_GROUPS, PACK], F32, name=name)
@@ -100,53 +107,56 @@ def tile_list_tree_ring_dating_kernel(
             for t in range(PACK):
                 nc.vector.memset(tree[g][t][:, M:], 0.0)
 
-        nc.sync.dma_start(w2_raw[:].bitcast(I32), w2_words.rearrange("a p c -> p a c").bitcast(I32))
-
-        w2_codes = keep.tile([P, H_GROUPS * H_GROUPS, PACK, 2 * P], U8, name="w2_codes", align_bytes=64)
-        w2_planes = keep.tile([P, H_GROUPS * H_GROUPS, PACK, P], U8, name="w2_planes", align_bytes=64)
-        nc.vector.tensor_copy(
-            out=w2_codes[:].rearrange("p s t (q b) -> p s q t b", b=2),
-            in_=w2_raw[:].rearrange("p a (g q t b) -> p (a g) q t b", g=H_GROUPS, t=PACK, b=2),
-        )
-
-        v_scales = keep.tile([P, S], U8, name="v_scales", align_bytes=64)
-        nc.vector.tensor_copy(v_scales[:], tab_scale_rows[:].indirect(offs_t[:]))
-        w2_scale_rows = ring.tile([P, H_GROUPS, H], U8, name="w2_scale_rows", tag="scale_rows", align_bytes=64)
-        nc.vector.memset(w2_scale_rows[:].bitcast(I32), 0)
+        tables = [load_table(0)]
         for q in range(4):
-            nc.scalar.dma_start(
+            nc.sync.dma_start(
+                tab_scale_rows[32 * q:32 * q + 4 * K_PASSES, :].bitcast(I32),
+                tab_scales[:, 4 * q:4 * q + 4, :].bitcast(I32),
+            )
+        nc.sync.dma_start(w2_raw[:].bitcast(I32), w2_words.rearrange("a p c -> p a c").bitcast(I32))
+        w1_first = [load_w1(0, 0, 0, GROUP)]
+        tables.append(load_table(1))
+        for q in range(4):
+            nc.sync.dma_start(
                 w2_scale_rows[32 * q:32 * q + 4, :, :].bitcast(I32),
                 w2_scales[:, 4 * q:4 * q + 4, :].rearrange("a r c -> r a c").bitcast(I32),
             )
-        nc.vector.tensor_copy(
-            out=w2_planes[:].rearrange("p s t q -> p s q t"),
-            in_=w2_scale_rows[:].rearrange("p a (g q t) -> p (a g) q t", g=H_GROUPS, t=PACK),
-        )
+        w1_first.append(load_w1(0, 1, 0, GROUP))
+        tables.append(load_table(2))
+        pos1_t = load_list(pos1, "pos1_t")
+        pos2_t = load_list(pos2, "pos2_t")
+        b1_t = load_vector(b1, "b1_t")
+
+        v_scales = keep.tile([P, S], U8, name="v_scales", align_bytes=64)
         v_words = []
         w1_mx = [[mx_pair(GROUP, "w1_%d%d" % (g, a)) for a in range(K_PASSES)] for g in range(H_GROUPS)]
+        w2_codes = keep.tile([P, H_GROUPS * H_GROUPS, PACK, 2 * P], U8, name="w2_codes", align_bytes=64)
+        w2_planes = keep.tile([P, H_GROUPS * H_GROUPS, PACK, P], U8, name="w2_planes", align_bytes=64)
         for a in range(K_PASSES):
-            table = big([P, T], I32, "table%d" % a)
-            nc.sync.dma_start(table[:], tab_words[a].rearrange("p n t -> p (n t)").bitcast(I32))
             picked = keep.tile([P, S], U32, name="v_words%d" % a, align_bytes=64)
-            nc.vector.tensor_copy(picked[:], table[:].bitcast(U32).indirect(offs_t[:]))
+            nc.vector.tensor_copy(picked[:], tables[a][:].bitcast(U32).indirect(offs_t[:]))
             v_words.append(picked)
+            if a == 0:
+                nc.vector.tensor_copy(v_scales[:], tab_scale_rows[:].indirect(offs_t[:]))
             staged = weight_stage("w1_bf0%d" % a)
             if a < K_PASSES - 1:
-                rows = raw([P, PACK, GROUP], "w1_raw0%d" % a)
-                nc.sync.dma_start(rows[:], w1_rows(a, 0, GROUP))
-                deal(nc.scalar.copy, staged[:], rows[:], 0, P)
+                deal(nc.scalar.copy, staged[:], w1_first[a][:], 0, P)
                 quantize(w1_mx[0][a], staged[:], 0, GROUP)
             else:
                 for half, copy in enumerate((nc.scalar.copy, nc.vector.tensor_copy)):
-                    rows = raw([P, PACK, GROUP // 2], "w1_raw0%d%d" % (a, half))
-                    nc.sync.dma_start(rows[:], w1_rows(a, half * GROUP // 2, (half + 1) * GROUP // 2))
+                    rows = load_w1(0, a, half * GROUP // 2, (half + 1) * GROUP // 2)
                     deal(copy, staged[:], rows[:], half * P // 2, (half + 1) * P // 2)
                 for t in range(PACK):
                     quantize(w1_mx[0][a], staged[:, t * GROUP:(t + 1) * GROUP], t * P, P)
             if a == 0:
-                pos1_t = load_list(pos1, "pos1_t")
-                pos2_t = load_list(pos2, "pos2_t")
-                b1_t = load_vector(b1, "b1_t")
+                nc.vector.tensor_copy(
+                    out=w2_codes[:].rearrange("p s t (q b) -> p s q t b", b=2),
+                    in_=w2_raw[:].rearrange("p a (g q t b) -> p (a g) q t b", g=H_GROUPS, t=PACK, b=2),
+                )
+                nc.vector.tensor_copy(
+                    out=w2_planes[:].rearrange("p s t q -> p s q t"),
+                    in_=w2_scale_rows[:].rearrange("p a (g q t) -> p (a g) q t", g=H_GROUPS, t=PACK),
+                )
 
         h = [[keep.tile([P, S], F32, name="h%d%d" % (g, t)) for t in range(PACK)] for g in range(H_GROUPS)]
 
@@ -200,8 +210,7 @@ def tile_list_tree_ring_dating_kernel(
         stage1_products(0)
 
         for a in range(K_PASSES):
-            rows = raw([P, PACK, GROUP], "w1_raw1%d" % a)
-            nc.sync.dma_start(rows[:], w1_rows(a, GROUP, 2 * GROUP))
+            rows = load_w1(1, a, 0, GROUP)
             staged = weight_stage("w1_bf1%d" % a)
             deal(nc.scalar.copy, staged[:], rows[:], 0, P)
             quantize(w1_mx[1][a], staged[:], 0, GROUP)

@@ -107,20 +107,20 @@ def tile_list_tree_ring_dating_kernel(
             for t in range(PACK):
                 nc.vector.memset(tree[g][t][:, M:], 0.0)
 
+        nc.sync.dma_start(w2_raw[:].bitcast(I32), w2_words.rearrange("a p c -> p a c").bitcast(I32))
         tables = [load_table(0)]
         for q in range(4):
-            nc.sync.dma_start(
+            nc.gpsimd.dma_start(
                 tab_scale_rows[32 * q:32 * q + 4 * K_PASSES, :].bitcast(I32),
                 tab_scales[:, 4 * q:4 * q + 4, :].bitcast(I32),
             )
-        nc.sync.dma_start(w2_raw[:].bitcast(I32), w2_words.rearrange("a p c -> p a c").bitcast(I32))
-        w1_first = [load_w1(0, 0, 0, GROUP)]
-        tables.append(load_table(1))
         for q in range(4):
             nc.sync.dma_start(
                 w2_scale_rows[32 * q:32 * q + 4, :, :].bitcast(I32),
                 w2_scales[:, 4 * q:4 * q + 4, :].rearrange("a r c -> r a c").bitcast(I32),
             )
+        w1_first = [load_w1(0, 0, 0, GROUP)]
+        tables.append(load_table(1))
         w1_first.append(load_w1(0, 1, 0, GROUP))
         tables.append(load_table(2))
         pos1_t = load_list(pos1, "pos1_t")
@@ -150,12 +150,12 @@ def tile_list_tree_ring_dating_kernel(
                     quantize(w1_mx[0][a], staged[:, t * GROUP:(t + 1) * GROUP], t * P, P)
             if a == 0:
                 nc.vector.tensor_copy(
-                    out=w2_codes[:].rearrange("p s t (q b) -> p s q t b", b=2),
-                    in_=w2_raw[:].rearrange("p a (g q t b) -> p (a g) q t b", g=H_GROUPS, t=PACK, b=2),
+                    out=w2_codes[:].bitcast(U16),
+                    in_=w2_raw[:].bitcast(U16).rearrange("p a (g q t) -> p (a g) t q", g=H_GROUPS, t=PACK),
                 )
                 nc.vector.tensor_copy(
-                    out=w2_planes[:].rearrange("p s t q -> p s q t"),
-                    in_=w2_scale_rows[:].rearrange("p a (g q t) -> p (a g) q t", g=H_GROUPS, t=PACK),
+                    out=w2_planes[:],
+                    in_=w2_scale_rows[:].rearrange("p a (g q t) -> p (a g) t q", g=H_GROUPS, t=PACK),
                 )
 
         h = [[keep.tile([P, S], F32, name="h%d%d" % (g, t)) for t in range(PACK)] for g in range(H_GROUPS)]
@@ -198,9 +198,9 @@ def tile_list_tree_ring_dating_kernel(
             for op, name in ((ALU.max, "hi"), (ALU.min, "lo")):
                 both = small([P, PACK * M], BF16, "%s_bf%d" % (name, g))
                 nc.vector.tensor_tensor(
-                    out=both[:].rearrange("p (c i t) -> p c t i", i=4, t=PACK),
-                    in0=ha[:].rearrange("p t (c i) -> p c t i", i=4),
-                    in1=hb[:].rearrange("p t (c i) -> p c t i", i=4),
+                    out=both[:].rearrange("p (c i t) -> p c t i", i=2, t=PACK),
+                    in0=ha[:].rearrange("p t (c i) -> p c t i", i=2),
+                    in1=hb[:].rearrange("p t (c i) -> p c t i", i=2),
                     op=op,
                 )
                 staged.append(both)
@@ -267,15 +267,21 @@ def tile_list_tree_ring_dating_kernel(
             for first, width in Y_CHUNKS[g]:
                 cols = slice(first, first + width)
                 last = g == H_GROUPS - 1 and first + width == S
-                for t in range(PACK):
-                    x = ring.tile([P, width], F32, name="x%d%d%d" % (g, first, t), tag="x", bufs=4)
-                    nc.vector.tensor_copy(x[:], tree[g][t][:].indirect(pos3_t[:, first // 16:(first + width) // 16]))
-                    nc.vector.scalar_tensor_tensor(
-                        out=x[:], in0=h[g][t][:, cols], scalar=gain_t[:, g, t:t + 1], in1=x[:],
-                        op0=ALU.mult, op1=ALU.add,
-                    )
-                    nc.scalar.activation(y[:, t, cols], x[:], ACT.Gelu_apprx_tanh)
-                    nc.scalar.activation(y[:, t, cols], y[:, t, cols], ACT.Copy, scale=amp_t[:, g, t:t + 1])
+                picks = pos3_t[:, first // 16:(first + width) // 16]
+                for t0 in range(0, PACK, 2):
+                    x = small([P, 2, width], F32, "x%d%d%d" % (g, first, t0))
+                    pair = ((0, t0), (1, t0 + 1))
+                    for u, t in pair:
+                        nc.vector.tensor_copy(x[:, u, :], tree[g][t][:].indirect(picks))
+                    for u, t in pair:
+                        nc.vector.scalar_tensor_tensor(
+                            out=x[:, u, :], in0=h[g][t][:, cols], scalar=gain_t[:, g, t:t + 1], in1=x[:, u, :],
+                            op0=ALU.mult, op1=ALU.add,
+                        )
+                    for u, t in pair:
+                        nc.scalar.activation(y[:, t, cols], x[:, u, :], ACT.Gelu_apprx_tanh)
+                    for u, t in pair:
+                        nc.scalar.activation(y[:, t, cols], y[:, t, cols], ACT.Copy, scale=amp_t[:, g, t:t + 1])
                 nc.sync.dma_start(y_rows[:, :, cols], y[:, :, cols])
                 staged = small([P, PACK * width], BF16, "y_bf%d%d" % (g, first))
                 copy = nc.vector.tensor_copy if last else nc.scalar.copy

@@ -21,9 +21,19 @@ PACK = 4
 GROUP = P * PACK
 K_PASSES = K // GROUP
 H_GROUPS = H // GROUP
+QUADRANTS = 4
+QUADRANT = P // QUADRANTS
+SCALE_ROWS = 4
+PER_COLUMN = 16
 BANK = 512
+RUN = 4
+LINE_COLUMNS = 2
 TREE_PAD = 16
+STAGE_BUFS = 5
+X_BUFS = 3
 Y_CHUNKS = [[(0, 512), (512, 512)], [(0, 512), (512, 256), (768, 256)]]
+SCALAR_ROUNDS = (0, 512)
+VECTOR_SCALES = ((1, 2), (1, 3))
 
 
 def tile_list_tree_ring_dating_kernel(
@@ -37,19 +47,17 @@ def tile_list_tree_ring_dating_kernel(
         ring = ctx.enter_context(tc.tile_pool(name="ring", bufs=1))
         psum = ctx.enter_context(tc.psum_pool(name="psum", bufs=1))
 
-        def load_list(src, name):
-            tile = lists.tile(list(src.shape), U16, name=name)
-            nc.sync.dma_start(tile[:], src)
-            return tile
+        def big(place, shape, dtype, name):
+            return ring.tile(shape, dtype, name=name, tag="big%d" % place, align_bytes=64)
 
-        def big(shape, dtype, name):
-            return ring.tile(shape, dtype, name=name, tag="big", bufs=3, align_bytes=64)
+        def mid(place, shape, dtype, name):
+            return ring.tile(shape, dtype, name=name, tag="mid%d" % place, align_bytes=64)
 
-        def raw(shape, name, dtype=F32):
-            return ring.tile(shape, dtype, name=name, tag="raw", bufs=3, align_bytes=64)
+        def stage(shape, dtype, name):
+            return ring.tile(shape, dtype, name=name, tag="stage", bufs=STAGE_BUFS, align_bytes=64)
 
-        def small(shape, dtype, name):
-            return ring.tile(shape, dtype, name=name, tag="small", bufs=6, align_bytes=64)
+        def bank(index, name):
+            return psum.tile([P, BANK], F32, name=name, tag="bank%d" % index)
 
         def mx_pair(width, name):
             codes = keep.tile([P, width], U32, name=name + "_codes", align_bytes=64)
@@ -64,36 +72,26 @@ def tile_list_tree_ring_dating_kernel(
                 in_=staged,
             )
 
-        def deal(copy, staged, rows, m0, m1):
+        def deal(copy, staged, rows, q0, q1):
             copy(
-                out=staged.rearrange("p (t m j) -> p m j t", t=PACK, j=PACK)[:, m0:m1],
-                in_=rows.rearrange("p j (m t) -> p m j t", t=PACK),
+                out=staged.rearrange("p (t q j) -> p q j t", t=PACK, j=PACK)[:, q0:q1],
+                in_=rows.rearrange("p j (q t) -> p q j t", t=PACK),
             )
 
-        def weight_stage(name):
-            return small([P, PACK * GROUP], BF16, name)
-
-        def w1_rows(a, c0, c1):
-            return w1[a * GROUP:(a + 1) * GROUP, c0:c1].rearrange("(p j) c -> p j c", j=PACK)
-
-        def bank(i, name):
-            return psum.tile([P, BANK], F32, name=name, tag="bank%d" % i)
-
-        offs_t = load_list(offs, "offs_t")
-        tab_scale_rows = small([P, T], U8, "tab_scale_rows")
-        w2_scale_rows = small([P, H_GROUPS, H], U8, "w2_scale_rows")
-        w2_raw = small([P, H_GROUPS, 2 * H], U8, "w2_raw")
-        nc.vector.memset(tab_scale_rows[:].bitcast(I32), 0)
-        nc.vector.memset(w2_scale_rows[:].bitcast(I32), 0)
+        def load_list(src, name):
+            tile = lists.tile(list(src.shape), U16, name=name)
+            nc.sync.dma_start(tile[:], src)
+            return tile
 
         def load_table(a):
-            table = big([P, T], I32, "table%d" % a)
+            table = big(a, [P, T], I32, "table%d" % a)
             nc.sync.dma_start(table[:], tab_words[a].rearrange("p n t -> p (n t)").bitcast(I32))
             return table
 
-        def load_w1(g, a, c0, c1):
-            rows = raw([P, PACK, c1 - c0], "w1_raw%d%d%d" % (g, a, c0))
-            nc.sync.dma_start(rows[:], w1_rows(a, g * GROUP + c0, g * GROUP + c1))
+        def load_w1(place, g, a, c0, c1):
+            rows = mid(place, [P, PACK, c1 - c0], F32, "w1_rows%d%d%d" % (g, a, c0))
+            src = w1[a * GROUP:(a + 1) * GROUP, g * GROUP + c0:g * GROUP + c1]
+            nc.sync.dma_start(rows[:], src.rearrange("(p j) c -> p j c", j=PACK))
             return rows
 
         def load_vector(src, name):
@@ -101,6 +99,12 @@ def tile_list_tree_ring_dating_kernel(
             nc.sync.dma_start(vec[:], src.rearrange("(g p t) -> p g t", p=P, t=PACK))
             return vec
 
+        offs_t = load_list(offs, "offs_t")
+        tab_scale_rows = stage([P, T], U8, "tab_scale_rows")
+        w2_scale_rows = stage([P, H_GROUPS, H], U8, "w2_scale_rows")
+        w2_raw = stage([P, H_GROUPS, 2 * H], U8, "w2_raw")
+        nc.vector.memset(tab_scale_rows[:].bitcast(I32), 0)
+        nc.vector.memset(w2_scale_rows[:].bitcast(I32), 0)
         tree = [[keep.tile([P, M + TREE_PAD], F32, name="tree%d%d" % (g, t)) for t in range(PACK)]
                 for g in range(H_GROUPS)]
         for g in range(H_GROUPS):
@@ -109,19 +113,19 @@ def tile_list_tree_ring_dating_kernel(
 
         nc.sync.dma_start(w2_raw[:].bitcast(I32), w2_words.rearrange("a p c -> p a c").bitcast(I32))
         tables = [load_table(0)]
-        for q in range(4):
+        for quad in range(QUADRANTS):
             nc.gpsimd.dma_start(
-                tab_scale_rows[32 * q:32 * q + 4 * K_PASSES, :].bitcast(I32),
-                tab_scales[:, 4 * q:4 * q + 4, :].bitcast(I32),
+                tab_scale_rows[QUADRANT * quad:QUADRANT * quad + SCALE_ROWS * K_PASSES, :].bitcast(I32),
+                tab_scales[:, SCALE_ROWS * quad:SCALE_ROWS * (quad + 1), :].bitcast(I32),
             )
-        for q in range(4):
+        for quad in range(QUADRANTS):
             nc.sync.dma_start(
-                w2_scale_rows[32 * q:32 * q + 4, :, :].bitcast(I32),
-                w2_scales[:, 4 * q:4 * q + 4, :].rearrange("a r c -> r a c").bitcast(I32),
+                w2_scale_rows[QUADRANT * quad:QUADRANT * quad + SCALE_ROWS, :, :].bitcast(I32),
+                w2_scales[:, SCALE_ROWS * quad:SCALE_ROWS * (quad + 1), :].rearrange("a r c -> r a c").bitcast(I32),
             )
-        w1_first = [load_w1(0, 0, 0, GROUP)]
+        w1_first = [load_w1(0, 0, 0, 0, GROUP)]
         tables.append(load_table(1))
-        w1_first.append(load_w1(0, 1, 0, GROUP))
+        w1_first.append(load_w1(1, 0, 1, 0, GROUP))
         tables.append(load_table(2))
         pos1_t = load_list(pos1, "pos1_t")
         pos2_t = load_list(pos2, "pos2_t")
@@ -131,20 +135,20 @@ def tile_list_tree_ring_dating_kernel(
         v_words = []
         w1_mx = [[mx_pair(GROUP, "w1_%d%d" % (g, a)) for a in range(K_PASSES)] for g in range(H_GROUPS)]
         w2_codes = keep.tile([P, H_GROUPS * H_GROUPS, PACK, 2 * P], U8, name="w2_codes", align_bytes=64)
-        w2_planes = keep.tile([P, H_GROUPS * H_GROUPS, PACK, P], U8, name="w2_planes", align_bytes=64)
+        w2_dealt_scales = keep.tile([P, H_GROUPS * H_GROUPS, PACK, P], U8, name="w2_dealt_scales", align_bytes=64)
         for a in range(K_PASSES):
             picked = keep.tile([P, S], U32, name="v_words%d" % a, align_bytes=64)
             nc.vector.tensor_copy(picked[:], tables[a][:].bitcast(U32).indirect(offs_t[:]))
             v_words.append(picked)
             if a == 0:
                 nc.vector.tensor_copy(v_scales[:], tab_scale_rows[:].indirect(offs_t[:]))
-            staged = weight_stage("w1_bf0%d" % a)
+            staged = stage([P, PACK * GROUP], BF16, "w1_bf0%d" % a)
             if a < K_PASSES - 1:
                 deal(nc.scalar.copy, staged[:], w1_first[a][:], 0, P)
                 quantize(w1_mx[0][a], staged[:], 0, GROUP)
             else:
                 for half, copy in enumerate((nc.scalar.copy, nc.vector.tensor_copy)):
-                    rows = load_w1(0, a, half * GROUP // 2, (half + 1) * GROUP // 2)
+                    rows = load_w1((2 + half) % 3, 0, a, half * GROUP // 2, (half + 1) * GROUP // 2)
                     deal(copy, staged[:], rows[:], half * P // 2, (half + 1) * P // 2)
                 for t in range(PACK):
                     quantize(w1_mx[0][a], staged[:, t * GROUP:(t + 1) * GROUP], t * P, P)
@@ -154,33 +158,34 @@ def tile_list_tree_ring_dating_kernel(
                     in_=w2_raw[:].bitcast(U16).rearrange("p a (g q t) -> p (a g) t q", g=H_GROUPS, t=PACK),
                 )
                 nc.vector.tensor_copy(
-                    out=w2_planes[:],
+                    out=w2_dealt_scales[:],
                     in_=w2_scale_rows[:].rearrange("p a (g q t) -> p (a g) t q", g=H_GROUPS, t=PACK),
                 )
 
         h = [[keep.tile([P, S], F32, name="h%d%d" % (g, t)) for t in range(PACK)] for g in range(H_GROUPS)]
+        halves = S // BANK
 
-        def stage1_products(g):
-            acc = [[bank(2 * t + c, "h_acc%d%d%d" % (g, t, c)) for c in range(2)] for t in range(PACK)]
+        def make_h(g):
+            acc = [[bank(halves * t + c, "h_acc%d%d%d" % (g, t, c)) for c in range(halves)] for t in range(PACK)]
             for a in range(K_PASSES):
                 codes, scales = w1_mx[g][a]
                 for t in range(PACK):
-                    for c in range(2):
+                    for c in range(halves):
                         cols = slice(c * BANK, (c + 1) * BANK)
                         nc.tensor.matmul_mx(
                             out=acc[t][c][:],
                             lhsT=codes[:, t * P:(t + 1) * P].bitcast(FP8X4),
                             lhsT_scale=scales[:, t * P:(t + 1) * P],
                             rhs=v_words[a][:, cols].bitcast(FP8X4),
-                            rhs_scale=v_scales[4 * a:P, cols],
+                            rhs_scale=v_scales[SCALE_ROWS * a:P, cols],
                             start=(a == 0),
                             stop=(a == K_PASSES - 1),
                         )
             for t in range(PACK):
-                for c in range(2):
+                for c in range(halves):
                     cols = slice(c * BANK, (c + 1) * BANK)
                     bias = b1_t[:, g, t:t + 1]
-                    if g == 0 and t == 0 and c == 1:
+                    if (g, t, c) == (0, 0, 1):
                         nc.vector.tensor_scalar(h[g][t][:, cols], acc[t][c][:], bias, None, ALU.add)
                     else:
                         nc.scalar.activation(h[g][t][:, cols], acc[t][c][:], ACT.Identity, bias=bias, scale=1.0)
@@ -188,47 +193,62 @@ def tile_list_tree_ring_dating_kernel(
         hi_mx = [mx_pair(M, "hi%d" % g) for g in range(H_GROUPS)]
         lo_mx = [mx_pair(M, "lo%d" % g) for g in range(H_GROUPS)]
 
-        def pair_up(g):
-            ha = ring.tile([P, PACK, M], F32, name="ha%d" % g, tag="hab", bufs=2)
-            hb = ring.tile([P, PACK, M], F32, name="hb%d" % g, tag="hab", bufs=2)
+        def make_hi_lo(g):
+            ha = ring.tile([P, PACK, M], F32, name="ha%d" % g, tag="cores", bufs=2)
+            hb = ring.tile([P, PACK, M], F32, name="hb%d" % g, tag="cores", bufs=2)
             for t in range(PACK):
                 nc.vector.tensor_copy(ha[:, t, :], h[g][t][:].indirect(pos1_t[:]))
                 nc.vector.tensor_copy(hb[:, t, :], h[g][t][:].indirect(pos2_t[:]))
             staged = []
-            for op, name in ((ALU.max, "hi"), (ALU.min, "lo")):
-                both = small([P, PACK * M], BF16, "%s_bf%d" % (name, g))
+            for place, op, name in ((1, ALU.max, "hi"), (2, ALU.min, "lo")):
+                if g == 0:
+                    joined = stage([P, PACK * M], BF16, "%s_bf%d" % (name, g))
+                else:
+                    joined = mid(place, [P, PACK * M], BF16, "%s_bf%d" % (name, g))
                 nc.vector.tensor_tensor(
-                    out=both[:].rearrange("p (c i t) -> p c t i", i=2, t=PACK),
-                    in0=ha[:].rearrange("p t (c i) -> p c t i", i=2),
-                    in1=hb[:].rearrange("p t (c i) -> p c t i", i=2),
+                    out=joined[:].rearrange("p (c i t) -> p c t i", i=LINE_COLUMNS, t=PACK),
+                    in0=ha[:].rearrange("p t (c i) -> p c t i", i=LINE_COLUMNS),
+                    in1=hb[:].rearrange("p t (c i) -> p c t i", i=LINE_COLUMNS),
                     op=op,
                 )
-                staged.append(both)
+                staged.append(joined)
             quantize(hi_mx[g], staged[0][:], 0, M)
             quantize(lo_mx[g], staged[1][:], 0, M)
 
-        stage1_products(0)
+        make_h(0)
 
         for a in range(K_PASSES):
-            rows = load_w1(1, a, 0, GROUP)
-            staged = weight_stage("w1_bf1%d" % a)
+            rows = load_w1((1 + a) % 3, 1, a, 0, GROUP)
+            staged = stage([P, PACK * GROUP], BF16, "w1_bf1%d" % a)
             deal(nc.scalar.copy, staged[:], rows[:], 0, P)
             quantize(w1_mx[1][a], staged[:], 0, GROUP)
-        stage1_products(1)
-        pair_up(0)
+        make_h(1)
+        make_hi_lo(0)
         pos3_t = load_list(pos3, "pos3_t")
         gain_t = load_vector(gain, "gain_t")
         amp_t = load_vector(amp, "amp_t")
 
         w3_mx = [mx_pair(H, "w3_%d" % a) for a in range(H_GROUPS)]
         for a in range(H_GROUPS):
-            rows = big([P, PACK, H], F32, "w3_raw%d" % a)
+            rows = big(a, [P, PACK, H], F32, "w3_rows%d" % a)
             nc.sync.dma_start(rows[:], w3[a * GROUP:(a + 1) * GROUP, :].rearrange("(p j) c -> p j c", j=PACK))
-            staged = raw([P, H_GROUPS, PACK * GROUP], "w3_bf%d" % a, BF16)
+            staged = mid(1 + a, [P, H_GROUPS, PACK * GROUP], BF16, "w3_bf%d" % a)
             for g in range(H_GROUPS):
                 deal(nc.scalar.copy, staged[:, g, :], rows[:, :, g * GROUP:(g + 1) * GROUP], 0, P)
             quantize(w3_mx[a], staged[:].rearrange("p g c -> p (g c)"), 0, H)
-        pair_up(1)
+        make_hi_lo(1)
+
+        own0 = big(0, [P, PACK, S], F32, "own0")
+        own1a = mid(0, [P, 2, S], F32, "own1a")
+        own1b = mid(2, [P, 2, S], F32, "own1b")
+        own = [[own0[:, t, :] for t in range(PACK)],
+               [own1a[:, 0, :], own1a[:, 1, :], own1b[:, 0, :], own1b[:, 1, :]]]
+        for g in range(H_GROUPS):
+            for t in range(PACK):
+                if (g, t) in VECTOR_SCALES:
+                    nc.vector.tensor_scalar(own[g][t], h[g][t][:], gain_t[:, g, t:t + 1], None, ALU.mult)
+                else:
+                    nc.scalar.activation(own[g][t], h[g][t][:], ACT.Copy, scale=gain_t[:, g, t:t + 1])
 
         acc = [[bank(PACK * g + t, "tree_acc%d%d" % (g, t)) for t in range(PACK)] for g in range(H_GROUPS)]
         for a in range(H_GROUPS):
@@ -237,7 +257,7 @@ def tile_list_tree_ring_dating_kernel(
                     nc.tensor.matmul_mx(
                         out=acc[g][t][:],
                         lhsT=w2_codes[:, H_GROUPS * a + g, t, :].bitcast(FP4X4),
-                        lhsT_scale=w2_planes[:, H_GROUPS * a + g, t, :],
+                        lhsT_scale=w2_dealt_scales[:, H_GROUPS * a + g, t, :],
                         rhs=hi_mx[a][0][:].bitcast(FP8X4),
                         rhs_scale=hi_mx[a][1][:],
                         start=(a == 0),
@@ -260,39 +280,45 @@ def tile_list_tree_ring_dating_kernel(
         for g in range(H_GROUPS):
             for t in range(PACK):
                 nc.scalar.copy(tree[g][t][:, :M], acc[g][t][:])
-            y = big([P, PACK, S], F32, "y%d" % g)
-            y_mx = mx_pair(S, "y%d" % g)
+        y = [big(2 - g, [P, PACK, S], F32, "y%d" % g) for g in range(H_GROUPS)]
+        y_mx = [mx_pair(S, "y%d" % g) for g in range(H_GROUPS)]
+
+        def make_y(g, first, width):
+            cols = slice(first, first + width)
+            picks = pos3_t[:, first // PER_COLUMN:(first + width) // PER_COLUMN]
+            for t0 in range(0, PACK, 2):
+                x = ring.tile([P, 2, width], F32, name="x%d%d%d" % (g, first, t0), tag="x", bufs=X_BUFS)
+                pair = ((0, t0), (1, t0 + 1))
+                for u, t in pair:
+                    nc.vector.tensor_tensor(x[:, u, :], tree[g][t][:].indirect(picks), own[g][t][:, cols], ALU.add)
+                for u, t in pair:
+                    nc.scalar.activation(y[g][:, t, cols], x[:, u, :], ACT.Gelu_apprx_tanh)
+                for u, t in pair:
+                    nc.scalar.activation(y[g][:, t, cols], y[g][:, t, cols], ACT.Copy, scale=amp_t[:, g, t:t + 1])
             y_rows = out_0[g * GROUP:(g + 1) * GROUP, :].rearrange("(p t) c -> p t c", t=PACK)
+            nc.sync.dma_start(y_rows[:, :, cols], y[g][:, :, cols])
+
+        def store_quantised_y(g, first, width):
+            cols = slice(first, first + width)
+            staged = stage([P, PACK * width], BF16, "y_bf%d%d" % (g, first))
+            copy = nc.scalar.copy if (g, first) == SCALAR_ROUNDS else nc.vector.tensor_copy
+            copy(
+                out=staged[:].rearrange("p (c i t) -> p c t i", i=RUN, t=PACK),
+                in_=y[g][:, :, cols].rearrange("p t (c i) -> p c t i", i=RUN),
+            )
+            quantize(y_mx[g], staged[:], first, width)
             y_words = out_1[g].rearrange("p n t -> p (n t)").bitcast(I32)
-            for first, width in Y_CHUNKS[g]:
-                cols = slice(first, first + width)
-                last = g == H_GROUPS - 1 and first + width == S
-                picks = pos3_t[:, first // 16:(first + width) // 16]
-                for t0 in range(0, PACK, 2):
-                    x = small([P, 2, width], F32, "x%d%d%d" % (g, first, t0))
-                    pair = ((0, t0), (1, t0 + 1))
-                    for u, t in pair:
-                        nc.vector.tensor_copy(x[:, u, :], tree[g][t][:].indirect(picks))
-                    for u, t in pair:
-                        nc.vector.scalar_tensor_tensor(
-                            out=x[:, u, :], in0=h[g][t][:, cols], scalar=gain_t[:, g, t:t + 1], in1=x[:, u, :],
-                            op0=ALU.mult, op1=ALU.add,
-                        )
-                    for u, t in pair:
-                        nc.scalar.activation(y[:, t, cols], x[:, u, :], ACT.Gelu_apprx_tanh)
-                    for u, t in pair:
-                        nc.scalar.activation(y[:, t, cols], y[:, t, cols], ACT.Copy, scale=amp_t[:, g, t:t + 1])
-                nc.sync.dma_start(y_rows[:, :, cols], y[:, :, cols])
-                staged = small([P, PACK * width], BF16, "y_bf%d%d" % (g, first))
-                copy = nc.vector.tensor_copy if last else nc.scalar.copy
-                copy(
-                    out=staged[:].rearrange("p (c i t) -> p c t i", i=4, t=PACK),
-                    in_=y[:, :, cols].rearrange("p t (c i) -> p c t i", i=4),
-                )
-                quantize(y_mx, staged[:], first, width)
-                nc.sync.dma_start(y_words[:, cols], y_mx[0][:, cols].bitcast(I32))
-            for q in range(4):
-                nc.sync.dma_start(
-                    out_2[g, 4 * q:4 * q + 4, :].bitcast(I32),
-                    y_mx[1][32 * q:32 * q + 4, :].bitcast(I32),
-                )
+            nc.sync.dma_start(y_words[:, cols], y_mx[g][0][:, cols].bitcast(I32))
+            if first + width == S:
+                for quad in range(QUADRANTS):
+                    nc.sync.dma_start(
+                        out_2[g, SCALE_ROWS * quad:SCALE_ROWS * (quad + 1), :].bitcast(I32),
+                        y_mx[g][1][QUADRANT * quad:QUADRANT * quad + SCALE_ROWS, :].bitcast(I32),
+                    )
+
+        chunks = [(g, first, width) for g in range(H_GROUPS) for first, width in Y_CHUNKS[g]]
+        for i, chunk in enumerate(chunks):
+            make_y(*chunk)
+            if i > 0:
+                store_quantised_y(*chunks[i - 1])
+        store_quantised_y(*chunks[-1])

from contextlib import ExitStack

import concourse.mybir as mybir

K, H, T, S, M = 1536, 1024, 4096, 1024, 512
FLOPS = 2 * K * H * S + 2 * 2 * H * H * M

F32 = mybir.dt.float32
BF16 = mybir.dt.bfloat16
I32 = mybir.dt.int32
U32 = mybir.dt.uint32
U16 = mybir.dt.uint16
U8 = mybir.dt.uint8
FP8X4 = mybir.dt.float8_e4m3fn_x4
FP4X4 = mybir.dt.float4_e2m1fn_x4
ACT = mybir.ActivationFunctionType
ALU = mybir.AluOpType

P = 128
PACK = 4
GROUP = P * PACK
K_PASSES = K // GROUP
H_GROUPS = H // GROUP
QUADRANTS = 4
QUADRANT = P // QUADRANTS
SCALE_ROWS = 4
PER_COLUMN = 16
BANK = 512
RUN = 4
LINE_COLUMNS = 2
TREE_PAD = 16
STAGE_BUFS = 5
X_BUFS = 3
Y_CHUNKS = [[(0, 512), (512, 512)], [(0, 512), (512, 256), (768, 256)]]
SCALAR_ROUNDS = (0, 512)
VECTOR_SCALES = ((1, 2), (1, 3))


def tile_list_tree_ring_dating_kernel(
    tc, tab_words, tab_scales, offs, w1, b1, pos1, pos2, w2_words, w2_scales, w3, pos3, gain, amp,
    out_0, out_1, out_2,
):
    nc = tc.nc
    with ExitStack() as ctx:
        lists = ctx.enter_context(tc.tile_pool(name="lists", bufs=1))
        keep = ctx.enter_context(tc.tile_pool(name="keep", bufs=1))
        ring = ctx.enter_context(tc.tile_pool(name="ring", bufs=1))
        psum = ctx.enter_context(tc.psum_pool(name="psum", bufs=1))

        def big(place, shape, dtype, name):
            return ring.tile(shape, dtype, name=name, tag="big%d" % place, align_bytes=64)

        def mid(place, shape, dtype, name):
            return ring.tile(shape, dtype, name=name, tag="mid%d" % place, align_bytes=64)

        def stage(shape, dtype, name):
            return ring.tile(shape, dtype, name=name, tag="stage", bufs=STAGE_BUFS, align_bytes=64)

        def bank(index, name):
            return psum.tile([P, BANK], F32, name=name, tag="bank%d" % index)

        def mx_pair(width, name):
            codes = keep.tile([P, width], U32, name=name + "_codes", align_bytes=64)
            scales = keep.tile([P, width], U8, name=name + "_scales", align_bytes=64)
            return codes, scales

        def quantize(pair, staged, first, width):
            codes, scales = pair
            nc.vector.quantize_mx(
                out=codes[:, first:first + width].bitcast(FP8X4),
                scales=scales[:, first:first + width],
                in_=staged,
            )

        def deal(copy, staged, rows, q0, q1):
            copy(
                out=staged.rearrange("p (t q j) -> p q j t", t=PACK, j=PACK)[:, q0:q1],
                in_=rows.rearrange("p j (q t) -> p q j t", t=PACK),
            )

        def load_list(src, name):
            tile = lists.tile(list(src.shape), U16, name=name)
            nc.sync.dma_start(tile[:], src)
            return tile

        def load_table(a):
            table = big(a, [P, T], I32, "table%d" % a)
            nc.sync.dma_start(table[:], tab_words[a].rearrange("p n t -> p (n t)").bitcast(I32))
            return table

        def load_w1(place, g, a, c0, c1):
            rows = mid(place, [P, PACK, c1 - c0], F32, "w1_rows%d%d%d" % (g, a, c0))
            src = w1[a * GROUP:(a + 1) * GROUP, g * GROUP + c0:g * GROUP + c1]
            nc.sync.dma_start(rows[:], src.rearrange("(p j) c -> p j c", j=PACK))
            return rows

        def load_vector(src, name):
            vec = keep.tile([P, H_GROUPS, PACK], F32, name=name)
            nc.sync.dma_start(vec[:], src.rearrange("(g p t) -> p g t", p=P, t=PACK))
            return vec

        offs_t = load_list(offs, "offs_t")
        tab_scale_rows = stage([P, T], U8, "tab_scale_rows")
        w2_scale_rows = stage([P, H_GROUPS, H], U8, "w2_scale_rows")
        w2_raw = stage([P, H_GROUPS, 2 * H], U8, "w2_raw")
        nc.vector.memset(tab_scale_rows[:].bitcast(I32), 0)
        nc.vector.memset(w2_scale_rows[:].bitcast(I32), 0)
        tree = [[keep.tile([P, M + TREE_PAD], F32, name="tree%d%d" % (g, t)) for t in range(PACK)]
                for g in range(H_GROUPS)]
        for g in range(H_GROUPS):
            for t in range(PACK):
                nc.vector.memset(tree[g][t][:, M:], 0.0)

        nc.sync.dma_start(w2_raw[:].bitcast(I32), w2_words.rearrange("a p c -> p a c").bitcast(I32))
        tables = [load_table(0)]
        for quad in range(QUADRANTS):
            nc.gpsimd.dma_start(
                tab_scale_rows[QUADRANT * quad:QUADRANT * quad + SCALE_ROWS * K_PASSES, :].bitcast(I32),
                tab_scales[:, SCALE_ROWS * quad:SCALE_ROWS * (quad + 1), :].bitcast(I32),
            )
        for quad in range(QUADRANTS):
            nc.sync.dma_start(
                w2_scale_rows[QUADRANT * quad:QUADRANT * quad + SCALE_ROWS, :, :].bitcast(I32),
                w2_scales[:, SCALE_ROWS * quad:SCALE_ROWS * (quad + 1), :].rearrange("a r c -> r a c").bitcast(I32),
            )
        w1_first = [load_w1(0, 0, 0, 0, GROUP)]
        tables.append(load_table(1))
        w1_first.append(load_w1(1, 0, 1, 0, GROUP))
        tables.append(load_table(2))
        pos1_t = load_list(pos1, "pos1_t")
        pos2_t = load_list(pos2, "pos2_t")
        b1_t = load_vector(b1, "b1_t")

        v_scales = keep.tile([P, S], U8, name="v_scales", align_bytes=64)
        v_words = []
        w1_mx = [[mx_pair(GROUP, "w1_%d%d" % (g, a)) for a in range(K_PASSES)] for g in range(H_GROUPS)]
        w2_codes = keep.tile([P, H_GROUPS * H_GROUPS, PACK, 2 * P], U8, name="w2_codes", align_bytes=64)
        w2_dealt_scales = keep.tile([P, H_GROUPS * H_GROUPS, PACK, P], U8, name="w2_dealt_scales", align_bytes=64)
        for a in range(K_PASSES):
            picked = keep.tile([P, S], U32, name="v_words%d" % a, align_bytes=64)
            nc.vector.tensor_copy(picked[:], tables[a][:].bitcast(U32).indirect(offs_t[:]))
            v_words.append(picked)
            if a == 0:
                nc.vector.tensor_copy(v_scales[:], tab_scale_rows[:].indirect(offs_t[:]))
            staged = stage([P, PACK * GROUP], BF16, "w1_bf0%d" % a)
            if a < K_PASSES - 1:
                deal(nc.scalar.copy, staged[:], w1_first[a][:], 0, P)
                quantize(w1_mx[0][a], staged[:], 0, GROUP)
            else:
                for half, copy in enumerate((nc.scalar.copy, nc.vector.tensor_copy)):
                    rows = load_w1((2 + half) % 3, 0, a, half * GROUP // 2, (half + 1) * GROUP // 2)
                    deal(copy, staged[:], rows[:], half * P // 2, (half + 1) * P // 2)
                for t in range(PACK):
                    quantize(w1_mx[0][a], staged[:, t * GROUP:(t + 1) * GROUP], t * P, P)
            if a == 0:
                nc.vector.tensor_copy(
                    out=w2_codes[:].bitcast(U16),
                    in_=w2_raw[:].bitcast(U16).rearrange("p a (g q t) -> p (a g) t q", g=H_GROUPS, t=PACK),
                )
                nc.vector.tensor_copy(
                    out=w2_dealt_scales[:],
                    in_=w2_scale_rows[:].rearrange("p a (g q t) -> p (a g) t q", g=H_GROUPS, t=PACK),
                )

        h = [[keep.tile([P, S], F32, name="h%d%d" % (g, t)) for t in range(PACK)] for g in range(H_GROUPS)]
        halves = S // BANK

        def make_h(g):
            acc = [[bank(halves * t + c, "h_acc%d%d%d" % (g, t, c)) for c in range(halves)] for t in range(PACK)]
            for a in range(K_PASSES):
                codes, scales = w1_mx[g][a]
                for t in range(PACK):
                    for c in range(halves):
                        cols = slice(c * BANK, (c + 1) * BANK)
                        nc.tensor.matmul_mx(
                            out=acc[t][c][:],
                            lhsT=codes[:, t * P:(t + 1) * P].bitcast(FP8X4),
                            lhsT_scale=scales[:, t * P:(t + 1) * P],
                            rhs=v_words[a][:, cols].bitcast(FP8X4),
                            rhs_scale=v_scales[SCALE_ROWS * a:P, cols],
                            start=(a == 0),
                            stop=(a == K_PASSES - 1),
                        )
            for t in range(PACK):
                for c in range(halves):
                    cols = slice(c * BANK, (c + 1) * BANK)
                    bias = b1_t[:, g, t:t + 1]
                    if (g, t, c) == (0, 0, 1):
                        nc.vector.tensor_scalar(h[g][t][:, cols], acc[t][c][:], bias, None, ALU.add)
                    else:
                        nc.scalar.activation(h[g][t][:, cols], acc[t][c][:], ACT.Identity, bias=bias, scale=1.0)

        hi_mx = [mx_pair(M, "hi%d" % g) for g in range(H_GROUPS)]
        lo_mx = [mx_pair(M, "lo%d" % g) for g in range(H_GROUPS)]

        def make_hi_lo(g):
            ha = ring.tile([P, PACK, M], F32, name="ha%d" % g, tag="cores", bufs=2)
            hb = ring.tile([P, PACK, M], F32, name="hb%d" % g, tag="cores", bufs=2)
            for t in range(PACK):
                nc.vector.tensor_copy(ha[:, t, :], h[g][t][:].indirect(pos1_t[:]))
                nc.vector.tensor_copy(hb[:, t, :], h[g][t][:].indirect(pos2_t[:]))
            staged = []
            for place, op, name in ((1, ALU.max, "hi"), (2, ALU.min, "lo")):
                if g == 0:
                    joined = stage([P, PACK * M], BF16, "%s_bf%d" % (name, g))
                else:
                    joined = mid(place, [P, PACK * M], BF16, "%s_bf%d" % (name, g))
                nc.vector.tensor_tensor(
                    out=joined[:].rearrange("p (c i t) -> p c t i", i=LINE_COLUMNS, t=PACK),
                    in0=ha[:].rearrange("p t (c i) -> p c t i", i=LINE_COLUMNS),
                    in1=hb[:].rearrange("p t (c i) -> p c t i", i=LINE_COLUMNS),
                    op=op,
                )
                staged.append(joined)
            quantize(hi_mx[g], staged[0][:], 0, M)
            quantize(lo_mx[g], staged[1][:], 0, M)

        make_h(0)

        for a in range(K_PASSES):
            rows = load_w1((1 + a) % 3, 1, a, 0, GROUP)
            staged = stage([P, PACK * GROUP], BF16, "w1_bf1%d" % a)
            deal(nc.scalar.copy, staged[:], rows[:], 0, P)
            quantize(w1_mx[1][a], staged[:], 0, GROUP)
        make_h(1)
        make_hi_lo(0)
        pos3_t = load_list(pos3, "pos3_t")
        gain_t = load_vector(gain, "gain_t")
        amp_t = load_vector(amp, "amp_t")

        w3_mx = [mx_pair(H, "w3_%d" % a) for a in range(H_GROUPS)]
        for a in range(H_GROUPS):
            rows = big(a, [P, PACK, H], F32, "w3_rows%d" % a)
            nc.sync.dma_start(rows[:], w3[a * GROUP:(a + 1) * GROUP, :].rearrange("(p j) c -> p j c", j=PACK))
            staged = mid(1 + a, [P, H_GROUPS, PACK * GROUP], BF16, "w3_bf%d" % a)
            for g in range(H_GROUPS):
                deal(nc.scalar.copy, staged[:, g, :], rows[:, :, g * GROUP:(g + 1) * GROUP], 0, P)
            quantize(w3_mx[a], staged[:].rearrange("p g c -> p (g c)"), 0, H)
        make_hi_lo(1)

        own0 = big(0, [P, PACK, S], F32, "own0")
        own1a = mid(0, [P, 2, S], F32, "own1a")
        own1b = mid(2, [P, 2, S], F32, "own1b")
        own = [[own0[:, t, :] for t in range(PACK)],
               [own1a[:, 0, :], own1a[:, 1, :], own1b[:, 0, :], own1b[:, 1, :]]]
        for g in range(H_GROUPS):
            for t in range(PACK):
                if (g, t) in VECTOR_SCALES:
                    nc.vector.tensor_scalar(own[g][t], h[g][t][:], gain_t[:, g, t:t + 1], None, ALU.mult)
                else:
                    nc.scalar.activation(own[g][t], h[g][t][:], ACT.Copy, scale=gain_t[:, g, t:t + 1])

        acc = [[bank(PACK * g + t, "tree_acc%d%d" % (g, t)) for t in range(PACK)] for g in range(H_GROUPS)]
        for a in range(H_GROUPS):
            for g in range(H_GROUPS):
                for t in range(PACK):
                    nc.tensor.matmul_mx(
                        out=acc[g][t][:],
                        lhsT=w2_codes[:, H_GROUPS * a + g, t, :].bitcast(FP4X4),
                        lhsT_scale=w2_dealt_scales[:, H_GROUPS * a + g, t, :],
                        rhs=hi_mx[a][0][:].bitcast(FP8X4),
                        rhs_scale=hi_mx[a][1][:],
                        start=(a == 0),
                        stop=False,
                    )
            for g in range(H_GROUPS):
                codes, scales = w3_mx[a]
                for t in range(PACK):
                    chans = slice((PACK * g + t) * P, (PACK * g + t + 1) * P)
                    nc.tensor.matmul_mx(
                        out=acc[g][t][:],
                        lhsT=codes[:, chans].bitcast(FP8X4),
                        lhsT_scale=scales[:, chans],
                        rhs=lo_mx[a][0][:].bitcast(FP8X4),
                        rhs_scale=lo_mx[a][1][:],
                        start=False,
                        stop=(a == H_GROUPS - 1),
                    )

        for g in range(H_GROUPS):
            for t in range(PACK):
                nc.scalar.copy(tree[g][t][:, :M], acc[g][t][:])
        y = [big(2 - g, [P, PACK, S], F32, "y%d" % g) for g in range(H_GROUPS)]
        y_mx = [mx_pair(S, "y%d" % g) for g in range(H_GROUPS)]

        def make_y(g, first, width):
            cols = slice(first, first + width)
            picks = pos3_t[:, first // PER_COLUMN:(first + width) // PER_COLUMN]
            for t0 in range(0, PACK, 2):
                x = ring.tile([P, 2, width], F32, name="x%d%d%d" % (g, first, t0), tag="x", bufs=X_BUFS)
                pair = ((0, t0), (1, t0 + 1))
                for u, t in pair:
                    nc.vector.tensor_tensor(x[:, u, :], tree[g][t][:].indirect(picks), own[g][t][:, cols], ALU.add)
                for u, t in pair:
                    nc.scalar.activation(y[g][:, t, cols], x[:, u, :], ACT.Gelu_apprx_tanh)
                for u, t in pair:
                    nc.scalar.activation(y[g][:, t, cols], y[g][:, t, cols], ACT.Copy, scale=amp_t[:, g, t:t + 1])
            y_rows = out_0[g * GROUP:(g + 1) * GROUP, :].rearrange("(p t) c -> p t c", t=PACK)
            nc.sync.dma_start(y_rows[:, :, cols], y[g][:, :, cols])

        def store_quantised_y(g, first, width):
            cols = slice(first, first + width)
            staged = stage([P, PACK * width], BF16, "y_bf%d%d" % (g, first))
            copy = nc.scalar.copy if (g, first) == SCALAR_ROUNDS else nc.vector.tensor_copy
            copy(
                out=staged[:].rearrange("p (c i t) -> p c t i", i=RUN, t=PACK),
                in_=y[g][:, :, cols].rearrange("p t (c i) -> p c t i", i=RUN),
            )
            quantize(y_mx[g], staged[:], first, width)
            y_words = out_1[g].rearrange("p n t -> p (n t)").bitcast(I32)
            nc.sync.dma_start(y_words[:, cols], y_mx[g][0][:, cols].bitcast(I32))
            if first + width == S:
                for quad in range(QUADRANTS):
                    nc.sync.dma_start(
                        out_2[g, SCALE_ROWS * quad:SCALE_ROWS * (quad + 1), :].bitcast(I32),
                        y_mx[g][1][QUADRANT * quad:QUADRANT * quad + SCALE_ROWS, :].bitcast(I32),
                    )

        chunks = [(g, first, width) for g in range(H_GROUPS) for first, width in Y_CHUNKS[g]]
        for i, chunk in enumerate(chunks):
            make_y(*chunk)
            if i > 0:
                store_quantised_y(*chunks[i - 1])
        store_quantised_y(*chunks[-1])
